import numpy as np
import ml_dtypes


def mxq(x, axis, fmt="e4m3"):
    dtype, down = {"e4m3": (ml_dtypes.float8_e4m3fn, 7), "e5m2": (ml_dtypes.float8_e5m2, 14)}[fmt]
    v = np.moveaxis(np.asarray(x, np.float32).astype(ml_dtypes.bfloat16).astype(np.float64), axis, -1)
    blocks = v.reshape(v.shape[:-1] + (-1, 32))
    amax = np.abs(blocks).max(-1, keepdims=True)
    byte = np.maximum(np.where(amax > 0, np.frexp(amax)[1] - 1 + 127, 0) - down, 1)
    scale = np.exp2(byte - 127.0)
    codes = (blocks / scale).astype(np.float32).astype(dtype).astype(np.float64)
    return np.moveaxis((codes * scale).reshape(v.shape), -1, axis)


WIDE = False


def mx_kscale(k):
    if not WIDE:
        return np.ones(k)
    levels = np.array([10, -10, 5, -5, 0])
    if k % 512:
        return np.exp2(np.random.permutation(np.resize(levels, k // 32))).repeat(32)
    a = np.empty((k // 512, 16))
    for p in range(k // 512):
        a[p, :8] = np.random.permutation(np.resize(levels, 8))
        for g in range(8):
            far = levels[np.abs(levels - a[p, g]) >= 10]
            a[p, g + 8] = far[np.random.randint(len(far))]
    return np.exp2(a.ravel()).repeat(32)


def f64(x):
    return np.asarray(x).astype(np.float64)


def striped(idx):
    return np.tile(np.asarray(idx).reshape(-1, 16).T, (8, 1)).astype(np.uint16)


def unstriped(offs):
    return offs[:16].T.reshape(-1).astype(np.int64)


E2M1 = np.array([0.0, 0.5, 1.0, 1.5, 2.0, 3.0, 4.0, 6.0, -0.0, -0.5, -1.0, -1.5, -2.0, -3.0, -4.0, -6.0])


def pack_weight(w, fmt):
    k, n = w.shape
    w = f64(np.asarray(w, np.float32).astype(ml_dtypes.bfloat16)).reshape(k // 32, 32, n)
    amax = np.abs(w).max(1)
    if fmt == "e4m3":
        byte = np.frexp(amax)[1] - 1 + 127 - 7
    else:
        mant, ex = np.frexp(amax / 6.0)
        byte = np.where(mant > 0.5, ex, ex - 1) + 127
    byte = np.clip(np.where(amax > 0, byte, 1), 1, 254)
    scaled = (w * np.exp2(127.0 - byte)[:, None, :]).reshape(k, n).astype(np.float32)
    by_word = np.ascontiguousarray(scaled.reshape(k // 512, 128, 4, n).transpose(0, 1, 3, 2))
    if fmt == "e4m3":
        words = by_word.astype(ml_dtypes.float8_e4m3fn).view(np.uint8)
    else:
        c = by_word.astype(ml_dtypes.float4_e2m1fn).view(np.uint8) & 0xF
        words = (c[..., 0::2] | (c[..., 1::2] << 4)).reshape(k // 512, 128, 2 * n)
    return np.ascontiguousarray(words), np.ascontiguousarray(byte.astype(np.uint8).reshape(k // 512, 16, n))


def unpack_weight(words, scales, fmt):
    g, _, n = scales.shape
    words = np.ascontiguousarray(words).reshape(g, 128, n, -1)
    if fmt == "e4m3":
        vals = words.view(ml_dtypes.float8_e4m3fn).astype(np.float64)
    else:
        nib = np.empty((g, 128, n, 4), np.uint8)
        nib[..., 0::2] = words & 0xF
        nib[..., 1::2] = words >> 4
        vals = E2M1[nib]
    vals = vals * np.repeat(np.exp2(scales.astype(np.float64) - 127.0), 8, axis=1)[..., None]
    return vals.transpose(0, 1, 3, 2).reshape(g * 512, n)


def sigmoid(v):
    return 1.0 / (1.0 + np.exp(-v))


def bf(x):
    return np.asarray(x, np.float32).astype(ml_dtypes.bfloat16)


def planes(Y):
    r, m = Y.shape
    b = f64(bf(Y)).reshape(r // 32, 32, m)
    amax = np.abs(b).max(1)
    byte = np.clip(np.where(amax > 0, np.frexp(amax)[1] - 1 + 127 - 7, 1), 1, 254)
    codes = (b * np.exp2(127.0 - byte)[:, None, :]).reshape(r, m).astype(np.float32).astype(ml_dtypes.float8_e4m3fn).view(np.uint8)
    words = codes.reshape(r // 512, 128, 4, m).transpose(0, 1, 3, 2)
    return np.ascontiguousarray(words), np.ascontiguousarray(byte.astype(np.uint8).reshape(r // 512, 16, m))


D, E, T, I, Q, G = 512, 512, 2048, 512, 256, 64


def setup_inputs():
    n = np.random.standard_normal
    idx = np.random.permutation(T)[:I]
    fd = mx_kscale(D)
    fi = mx_kscale(I)
    ti = np.ones(T)
    ti[idx] = fi
    keysp = pack_weight(n((D, T)) / fd[:, None], "e4m3")
    return {
        "query": (n((D, Q)) * 0.8 / np.sqrt(D) * fd[:, None]).astype(np.float32),
        "keys_words": keysp[0],
        "keys_scales": keysp[1],
        "th": (np.random.uniform(1.8, 2.8, (Q, 1))).astype(np.float32),
        "os": (np.random.uniform(0.1, 0.4, (1, I)) * fi).astype(np.float32),
        "vals": (n((E, T)) / ti).astype(np.float32),
        "offs": striped(idx),
    }


def reference(query, keys_words, keys_scales, th, os, vals, offs):
    idx = unstriped(offs)
    keysu = unpack_weight(keys_words, keys_scales, "e4m3")
    queryq = mxq(f64(query), 0, "e4m3")
    keysidxg = keysu[:, idx]
    a = queryq.T @ keysidxg
    p = np.exp(a)
    s = p.reshape(Q, G, I // G).sum(axis=2)
    sh = sigmoid(np.log(s) - f64(th)) / s
    sr = np.repeat(sh, I // G, axis=1)
    w = p * sr
    wo1 = w * f64(os)
    wt1 = wo1.T
    vt1 = f64(vals)[:, idx].T
    vt1q = mxq(vt1, 0, "e4m3")
    wt1q = mxq(wt1, 0, "e4m3")
    o = vt1q.T @ wt1q
    words, scales = planes(o)
    return o, words, scales

from contextlib import ExitStack

import concourse.mybir as mybir
from concourse.masks import make_identity

D, E, T, I, Q, G = 512, 512, 2048, 512, 256, 64
FLOPS = 2 * D * Q * I + 2 * I * E * Q

F32 = mybir.dt.float32
BF16 = mybir.dt.bfloat16
I32 = mybir.dt.int32
U32 = mybir.dt.uint32
U16 = mybir.dt.uint16
U8 = mybir.dt.uint8
FP8X4 = mybir.dt.float8_e4m3fn_x4
ACT = mybir.ActivationFunctionType
ALU = mybir.AluOpType

P = 128
PACK = 4
Q_TILES = Q // P
LIST_COLS = I // 16


def tile_attend_gatedgroups_pl_kernel(tc, query, keys_words, keys_scales, th, slot_factor, vals, offs, out_0, out_1, out_2):
    nc = tc.nc
    with ExitStack() as ctx:
        keep = ctx.enter_context(tc.tile_pool(name="keep", bufs=1))
        psum = ctx.enter_context(tc.psum_pool(name="psum", bufs=1))

        offsets = keep.tile([P, LIST_COLS], U16, name="offsets")
        nc.sync.dma_start(offsets[:], offs)

        query_raw = keep.tile([P, PACK, Q], F32, name="query_raw")
        nc.sync.dma_start(query_raw[:], query.rearrange("(p t) q -> p t q", t=PACK))

        key_scale_pool = keep.tile([P, T], U8, name="key_scale_pool")
        nc.gpsimd.memset(key_scale_pool[:].bitcast(I32), 0)
        for quad in range(4):
            nc.sync.dma_start(
                key_scale_pool[32 * quad : 32 * quad + 4, :].bitcast(I32),
                keys_scales[0, 4 * quad : 4 * quad + 4, :].bitcast(I32),
            )

        key_word_pool = keep.tile([P, T], U32, name="key_word_pool")
        nc.sync.dma_start(key_word_pool[:].bitcast(I32), keys_words[0].rearrange("p n t -> p (n t)").bitcast(I32))

        vals_planes = vals.rearrange("(p t) n -> p t n", t=PACK)
        val_pool = []

        def load_plane(t):
            plane = keep.tile([P, T], F32, name="val_pool%d" % t, tag="val_pool%d" % t, align_bytes=64)
            nc.sync.dma_start(plane[:], vals_planes[:, t, :])
            val_pool.append(plane)

        load_plane(0)
        th_col = keep.tile([P, Q_TILES], F32, name="th_col")
        with nc.allow_non_contiguous_dma(reason="one threshold a partition for each query tile"):
            nc.sync.dma_start(th_col[:], th.rearrange("(j p) o -> p (j o)", p=P))
        os_col = keep.tile([P, PACK], F32, name="os_col")
        nc.sync.dma_start(os_col[:], slot_factor.rearrange("o (s r) -> s (o r)", r=PACK))

        for t in range(1, PACK):
            load_plane(t)

        ident = keep.tile([P, P], F32, name="ident")
        make_identity(nc, ident[:])

        exp_th = keep.tile([P, Q_TILES], F32, name="exp_th")
        nc.scalar.activation(exp_th[:], th_col[:], ACT.Exp)

        q_operands = []
        for j in range(Q_TILES):
            q_bf = keep.tile([P, P * PACK], BF16, name="q_bf%d" % j, align_bytes=64)
            dst = q_bf[:].rearrange("p (c i t) -> p c t i", i=4, t=PACK)
            src = query_raw[:, :, j * P : (j + 1) * P].rearrange("p t (c i) -> p c t i", i=4)
            if j == 0:
                nc.vector.tensor_copy(dst, src)
            else:
                nc.scalar.copy(dst, src)
            q_codes = keep.tile([P, P], U32, name="q_codes%d" % j, align_bytes=64)
            q_scales = keep.tile([P, P], U8, name="q_scales%d" % j, align_bytes=64)
            nc.vector.quantize_mx(out=q_codes[:].bitcast(FP8X4), scales=q_scales[:], in_=q_bf[:])
            q_operands.append((q_codes, q_scales))

        key_scales = keep.tile([P, I], U8, name="key_scales", align_bytes=64)
        nc.vector.tensor_copy(key_scales[:], key_scale_pool[:].indirect(offsets[:]))
        key_words = keep.tile([P, I], U32, name="key_words", align_bytes=64)
        nc.vector.tensor_copy(key_words[:], key_word_pool[:].indirect(offsets[:]))

        scores = []
        for j, (q_codes, q_scales) in enumerate(q_operands):
            score = psum.tile([P, I], F32, name="score%d" % j, tag="score%d" % j)
            nc.tensor.matmul_mx(
                out=score[:],
                lhsT=q_codes[:].bitcast(FP8X4),
                lhsT_scale=q_scales[:],
                rhs=key_words[:].bitcast(FP8X4),
                rhs_scale=key_scales[:],
                start=True,
                stop=True,
            )
            scores.append(score)

        w_codes = []
        w_scales = []
        for j in range(Q_TILES):
            p_exp = keep.tile([P, 2, P, 2], F32, name="p_exp%d" % j)
            nc.scalar.activation(p_exp[:], scores[j][:].rearrange("q (s u e) -> q u s e", u=2, e=2), ACT.Exp)
            group_sum = keep.tile([P, G], F32, name="group_sum%d" % j)
            nc.vector.tensor_reduce(
                out=group_sum[:],
                in_=p_exp[:].rearrange("q u (g h) e -> q g u (h e)", h=2),
                axis=mybir.AxisListType.XY,
                op=ALU.add,
            )
            denom = keep.tile([P, G], F32, name="denom%d" % j)
            nc.vector.tensor_scalar(denom[:], group_sum[:], exp_th[:, j : j + 1], None, ALU.add)
            share = keep.tile([P, G], F32, name="share%d" % j)
            nc.vector.reciprocal(share[:], denom[:])
            w = keep.tile([P, 2, P, 2], F32, name="w%d" % j)
            nc.vector.tensor_tensor(
                w[:].rearrange("q u (g h) e -> q u g (h e)", h=2),
                p_exp[:].rearrange("q u (g h) e -> q u g (h e)", h=2),
                share[:].unsqueeze(1).unsqueeze(3).to_broadcast([P, 2, G, 4]),
                ALU.mult,
            )
            w_turned = psum.tile([P, PACK, P], F32, name="w_turned%d" % j)
            for r in range(PACK):
                nc.tensor.transpose(w_turned[:, r, :], w[:, r // 2, :, r % 2], ident[:])
            w_bf = keep.tile([P, P * PACK], BF16, name="w_bf%d" % j, align_bytes=64)
            nc.vector.tensor_tensor(
                w_bf[:].rearrange("s (q r) -> s q r", r=PACK),
                w_turned[:].rearrange("s r q -> s q r"),
                os_col[:].unsqueeze(1).to_broadcast([P, P, PACK]),
                ALU.mult,
            )
            codes = keep.tile([P, P], U32, name="w_codes%d" % j, align_bytes=64)
            scales = keep.tile([P, P], U8, name="w_scales%d" % j, align_bytes=64)
            nc.vector.quantize_mx(out=codes[:].bitcast(FP8X4), scales=scales[:], in_=w_bf[:])
            w_codes.append(codes)
            w_scales.append(scales)

        results = []
        out_planes = out_0.rearrange("(p t) q -> p t q", t=PACK)

        def store_planes(first, count, tag):
            staged = keep.tile([P, count, Q], F32, name="staged%d" % first, tag=tag, align_bytes=64)
            for j in reversed(range(Q_TILES)):
                dst = staged[:, :, j * P : (j + 1) * P]
                src = results[j][:, first : first + count, :]
                if j == 0 and first == 0:
                    nc.vector.tensor_copy(dst, src)
                else:
                    nc.scalar.copy(dst, src)
            nc.sync.dma_start(out_planes[:, first : first + count, :], staged[:])

        def gather_and_turn(t):
            picked = keep.tile([P, I], BF16, name="picked%d" % t)
            nc.scalar.activation(picked[:], val_pool[t][:].indirect(offsets[:]), ACT.Copy)
            pairs = picked[:].bitcast(F32).rearrange("p (s u) -> p u s", u=2)
            v_turned = psum.tile([P, 2, P], F32, name="v_turned%d" % t, tag=("turn_a", "turn_b", "turn_a", "score0")[t])
            for u in range(2):
                nc.tensor.transpose(v_turned[:, u, :], pairs[:, u, :], ident[:])
            return v_turned

        def quantise_plane(t, v_turned, tag):
            v_bf = keep.tile([P, P * PACK], BF16, name="v_bf%d" % t, tag=tag, align_bytes=64)
            nc.scalar.copy(
                v_bf[:].bitcast(F32).rearrange("s (e u) -> s e u", u=2),
                v_turned[:].rearrange("s u e -> s e u"),
            )
            v_codes = keep.tile([P, P], U32, name="v_codes%d" % t, align_bytes=64)
            v_scales = keep.tile([P, P], U8, name="v_scales%d" % t, align_bytes=64)
            nc.vector.quantize_mx(out=v_codes[:].bitcast(FP8X4), scales=v_scales[:], in_=v_bf[:])
            return v_codes, v_scales

        def multiply(t, v_codes, v_scales):
            for j in range(Q_TILES):
                nc.tensor.matmul_mx(
                    out=results[j][:, t, :],
                    lhsT=v_codes[:].bitcast(FP8X4),
                    lhsT_scale=v_scales[:],
                    rhs=w_codes[j][:].bitcast(FP8X4),
                    rhs_scale=w_scales[j][:],
                    start=True,
                    stop=True,
                )

        operands = [quantise_plane(0, gather_and_turn(0), "v_bf0")]
        turned_1 = gather_and_turn(1)
        turned_2 = gather_and_turn(2)
        operands.append(quantise_plane(1, turned_1, "val_pool2"))
        operands.append(quantise_plane(2, turned_2, "v_bf2"))
        turned_3 = gather_and_turn(3)
        for j, tag in enumerate(("turn_a", "turn_b")):
            results.append(psum.tile([P, PACK, P], F32, name="result%d" % j, tag=tag))
        for t in range(PACK - 1):
            multiply(t, *operands[t])
        last = quantise_plane(3, turned_3, "v_bf3")
        store_planes(0, PACK - 1, "val_pool3")
        multiply(3, *last)

        y_codes = keep.tile([P, Q], U32, name="y_codes", align_bytes=64)
        y_scales = keep.tile([P, Q], U8, name="y_scales", align_bytes=64)
        y_bf = []
        for j in range(Q_TILES):
            rounded = keep.tile([P, P * PACK], BF16, name="y_bf%d" % j, align_bytes=64)
            dst = rounded[:].rearrange("p (q t) -> p q t", t=PACK)
            src = results[j][:].rearrange("p t q -> p q t")
            if j == 0:
                nc.vector.tensor_copy(dst, src)
            else:
                nc.scalar.copy(dst, src)
            y_bf.append(rounded)
        store_planes(PACK - 1, 1, "staged_last")
        for j in reversed(range(Q_TILES)):
            cols = slice(j * P, (j + 1) * P)
            nc.vector.quantize_mx(out=y_codes[:, cols].bitcast(FP8X4), scales=y_scales[:, cols], in_=y_bf[j][:])
        nc.sync.dma_start(out_1[0].rearrange("p n t -> p (n t)").bitcast(I32), y_codes[:].bitcast(I32))
        for quad in range(4):
            queue = nc.sync if quad % 2 == 0 else nc.scalar
            queue.dma_start(
                out_2[0, 4 * quad : 4 * quad + 4, :].bitcast(I32),
                y_scales[32 * quad : 32 * quad + 4, :].bitcast(I32),
            )
